import numpy as np
import ml_dtypes


def mxq(x, axis, fmt="e4m3"):
    dtype, down = {"e4m3": (ml_dtypes.float8_e4m3fn, 7), "e5m2": (ml_dtypes.float8_e5m2, 14)}[fmt]
    v = np.moveaxis(np.asarray(x, np.float32).astype(ml_dtypes.bfloat16).astype(np.float64), axis, -1)
    blocks = v.reshape(v.shape[:-1] + (-1, 32))
    amax = np.abs(blocks).max(-1, keepdims=True)
    byte = np.maximum(np.where(amax > 0, np.frexp(amax)[1] - 1 + 127, 0) - down, 1)
    scale = np.exp2(byte - 127.0)
    codes = (blocks / scale).astype(np.float32).astype(dtype).astype(np.float64)
    return np.moveaxis((codes * scale).reshape(v.shape), -1, axis)


WIDE = False


def mx_kscale(k):
    if not WIDE:
        return np.ones(k)
    levels = np.array([10, -10, 5, -5, 0])
    if k % 512:
        return np.exp2(np.random.permutation(np.resize(levels, k // 32))).repeat(32)
    a = np.empty((k // 512, 16))
    for p in range(k // 512):
        a[p, :8] = np.random.permutation(np.resize(levels, 8))
        for g in range(8):
            far = levels[np.abs(levels - a[p, g]) >= 10]
            a[p, g + 8] = far[np.random.randint(len(far))]
    return np.exp2(a.ravel()).repeat(32)


def f64(x):
    return np.asarray(x).astype(np.float64)


def striped8(idx):
    return np.asarray(idx).reshape(8, -1, 16).transpose(0, 2, 1).reshape(128, -1).astype(np.uint16)


def unstriped8(offs):
    return offs.reshape(8, 16, -1).transpose(0, 2, 1).reshape(8, -1).astype(np.int64)


def pick8(x, idx, run):
    r = np.arange(len(x))
    return x[r[:, None], idx[r % (8 * run) // run]]


E2M1 = np.array([0.0, 0.5, 1.0, 1.5, 2.0, 3.0, 4.0, 6.0, -0.0, -0.5, -1.0, -1.5, -2.0, -3.0, -4.0, -6.0])


def pack_weight(w, fmt):
    k, n = w.shape
    w = f64(np.asarray(w, np.float32).astype(ml_dtypes.bfloat16)).reshape(k // 32, 32, n)
    amax = np.abs(w).max(1)
    if fmt == "e4m3":
        byte = np.frexp(amax)[1] - 1 + 127 - 7
    else:
        mant, ex = np.frexp(amax / 6.0)
        byte = np.where(mant > 0.5, ex, ex - 1) + 127
    byte = np.clip(np.where(amax > 0, byte, 1), 1, 254)
    scaled = (w * np.exp2(127.0 - byte)[:, None, :]).reshape(k, n).astype(np.float32)
    by_word = np.ascontiguousarray(scaled.reshape(k // 512, 128, 4, n).transpose(0, 1, 3, 2))
    if fmt == "e4m3":
        words = by_word.astype(ml_dtypes.float8_e4m3fn).view(np.uint8)
    else:
        c = by_word.astype(ml_dtypes.float4_e2m1fn).view(np.uint8) & 0xF
        words = (c[..., 0::2] | (c[..., 1::2] << 4)).reshape(k // 512, 128, 2 * n)
    return np.ascontiguousarray(words), np.ascontiguousarray(byte.astype(np.uint8).reshape(k // 512, 16, n))


def unpack_weight(words, scales, fmt):
    g, _, n = scales.shape
    words = np.ascontiguousarray(words).reshape(g, 128, n, -1)
    if fmt == "e4m3":
        vals = words.view(ml_dtypes.float8_e4m3fn).astype(np.float64)
    else:
        nib = np.empty((g, 128, n, 4), np.uint8)
        nib[..., 0::2] = words & 0xF
        nib[..., 1::2] = words >> 4
        vals = E2M1[nib]
    vals = vals * np.repeat(np.exp2(scales.astype(np.float64) - 127.0), 8, axis=1)[..., None]
    return vals.transpose(0, 1, 3, 2).reshape(g * 512, n)


D, T, I, Q = 512, 1024, 512, 128


def setup_inputs():
    n = np.random.standard_normal
    idx = np.stack([np.random.permutation(T)[:I] for _ in range(8)])
    idx2 = np.stack([np.random.permutation(T)[:I] for _ in range(8)])
    idx3 = np.stack([np.random.permutation(T)[:I] for _ in range(8)])
    fd = mx_kscale(D)
    keysp = pack_weight(n((D, T)) / fd[:, None], "e4m3")
    return {
        "query": (n((D, Q)) * 1.0 / np.sqrt(D) * fd[:, None]).astype(np.float32),
        "keys_words": keysp[0],
        "keys_scales": keysp[1],
        "old": (1.0 * n((Q, T))).astype(np.float32),
        "offs": striped8(idx),
        "offs2": striped8(idx2),
        "offs3": striped8(idx3),
    }


def reference(query, keys_words, keys_scales, old, offs, offs2, offs3):
    idx = unstriped8(offs)
    idx2 = unstriped8(offs2)
    idx3 = unstriped8(offs3)
    keysu = unpack_weight(keys_words, keys_scales, "e4m3")
    queryq = mxq(f64(query), 0, "e4m3")
    a = queryq.T @ keysu
    w = pick8(a, idx, 16) * pick8(a, idx2, 16)
    f1 = np.zeros((Q, T))
    f1[np.arange(Q)[:, None], idx3[np.arange(Q) % 128 // 16]] = w
    y = np.maximum(f1, f64(old)) + f64(old) * 0.25
    return y

@@ -1,0 +1,108 @@
+from contextlib import ExitStack
+
+import concourse.mybir as mybir
+
+D, T, I, Q = 512, 1024, 512, 128
+FLOPS = 2 * D * T * Q
+
+F32 = mybir.dt.float32
+BF16 = mybir.dt.bfloat16
+I32 = mybir.dt.int32
+U32 = mybir.dt.uint32
+U16 = mybir.dt.uint16
+U8 = mybir.dt.uint8
+FP8X4 = mybir.dt.float8_e4m3fn_x4
+ALU = mybir.AluOpType
+COPY = mybir.ActivationFunctionType.Copy
+
+P = 128
+PACK = 4
+HALF_T = T // 2
+HALF_I = I // 2
+LIST_COLS = I // 16
+OUT_CHUNK = 256
+
+
+def tile_attend_pairproduct_lean_largerput_heads_kernel(tc, query, keys_words, keys_scales, old, offs, offs2, offs3, out):
+    nc = tc.nc
+    with ExitStack() as ctx:
+        sb = ctx.enter_context(tc.tile_pool(name="sb", bufs=1))
+        ps = ctx.enter_context(tc.psum_pool(name="ps", bufs=1))
+
+        q_raw = sb.tile([P, PACK, Q], F32, name="q_raw")
+        nc.sync.dma_start(out=q_raw[:], in_=query.rearrange("(p j) q -> p j q", j=PACK))
+
+        k_scales = sb.tile([P, T], U8, name="k_scales", align_bytes=64)
+        scale_rows = keys_scales[0].bitcast(I32)
+        for quad in range(4):
+            nc.sync.dma_start(out=k_scales[32 * quad : 32 * quad + 4, :].bitcast(I32), in_=scale_rows[4 * quad : 4 * quad + 4, :])
+
+        word_rows = keys_words[0].rearrange("p t r -> p (t r)").bitcast(I32)
+        k_words = []
+        for h in range(2):
+            kw = sb.tile([P, HALF_T], U32, name=f"k_words{h}", align_bytes=64)
+            nc.sync.dma_start(out=kw[:].bitcast(I32), in_=word_rows[:, h * HALF_T : (h + 1) * HALF_T])
+            k_words.append(kw)
+
+        lists = []
+        for name, src in (("list1", offs), ("list2", offs2), ("list3", offs3)):
+            lt = sb.tile([P, LIST_COLS], U16, name=name)
+            nc.sync.dma_start(lt[:], src)
+            lists.append(lt)
+        list1, list2, list3 = lists
+
+        old_sb = sb.tile([P, T], F32, name="old_sb")
+        nc.sync.dma_start(out=old_sb[:], in_=old)
+
+        f1 = sb.tile([P, T], F32, name="f1")
+        nc.vector.memset(f1[:], 0.0)
+
+        q_bf = sb.tile([P, Q, PACK], BF16, name="q_bf", align_bytes=64)
+        q_codes = sb.tile([P, Q], U32, name="q_codes", align_bytes=64)
+        q_scales = sb.tile([P, Q], U8, name="q_scales", align_bytes=64)
+        nc.vector.tensor_copy(out=q_bf[:], in_=q_raw[:].rearrange("p j q -> p q j"))
+        nc.vector.quantize_mx(out=q_codes[:].bitcast(FP8X4), scales=q_scales[:], in_=q_bf[:].rearrange("p q j -> p (q j)"))
+
+        a = sb.tile([P, T], F32, name="a")
+        pieces = ((0, 512, "s"), (512, 256, "v"), (768, 128, "v"), (896, 128, "s"))
+        for n, (t0, width, eng) in enumerate(pieces):
+            bank = ps.tile([P, width], F32, name=f"bank{n}")
+            h, c0 = divmod(t0, HALF_T)
+            nc.tensor.matmul_mx(
+                out=bank[:],
+                lhsT=q_codes[:].bitcast(FP8X4),
+                lhsT_scale=q_scales[:],
+                rhs=k_words[h][:, c0 : c0 + width].bitcast(FP8X4),
+                rhs_scale=k_scales[:, t0 : t0 + width],
+                start=True,
+                stop=True,
+            )
+            if eng == "s":
+                nc.scalar.activation(a[:, t0 : t0 + width], bank[:], COPY)
+            else:
+                nc.vector.tensor_copy(a[:, t0 : t0 + width], bank[:])
+
+        half_cols = LIST_COLS // 2
+        for h in range(2):
+            cols = slice(h * half_cols, (h + 1) * half_cols)
+            left = sb.tile([P, HALF_I], F32, name=f"left{h}")
+            right = sb.tile([P, HALF_I], F32, name=f"right{h}")
+            nc.scalar.activation(left[:], a[:].indirect(list1[:, cols]), COPY)
+            if h == 0:
+                nc.vector.tensor_copy(right[:], a[:].indirect(list2[:, cols]))
+            else:
+                nc.scalar.activation(right[:], a[:].indirect(list2[:, cols]), COPY)
+            nc.vector.tensor_tensor(f1[:].indirect(list3[:, cols]), left[:], right[:], ALU.mult)
+
+        n_chunks = T // OUT_CHUNK
+        larger = [sb.tile([P, OUT_CHUNK], F32, name=f"larger{c}") for c in range(n_chunks)]
+        result = [sb.tile([P, OUT_CHUNK], F32, name=f"result{c}") for c in range(n_chunks)]
+        for step in range(n_chunks + 1):
+            if step < n_chunks:
+                cols = slice(step * OUT_CHUNK, (step + 1) * OUT_CHUNK)
+                nc.vector.tensor_tensor(larger[step][:], f1[:, cols], old_sb[:, cols], ALU.max)
+            if step > 0:
+                c = step - 1
+                cols = slice(c * OUT_CHUNK, (c + 1) * OUT_CHUNK)
+                nc.vector.scalar_tensor_tensor(result[c][:], old_sb[:, cols], 0.25, larger[c][:], ALU.mult, ALU.add)
+                nc.sync.dma_start(out=out[:, cols], in_=result[c][:])

@@ -1,6 +1,7 @@
 from contextlib import ExitStack
 
 import concourse.mybir as mybir
+from concourse.masks import make_identity
 
 D, T, I, Q = 512, 1024, 512, 128
 FLOPS = 2 * D * T * Q
@@ -54,6 +55,9 @@ def tile_attend_pairproduct_lean_largerput_heads_kernel(tc, query, keys_words, k
         old_sb = sb.tile([P, T], F32, name="old_sb")
         nc.sync.dma_start(out=old_sb[:], in_=old)
 
+        ident = sb.tile([P, P], F32, name="ident")
+        make_identity(nc, ident[:])
+
         f1 = sb.tile([P, T], F32, name="f1")
         nc.vector.memset(f1[:], 0.0)
 
@@ -66,7 +70,7 @@ def tile_attend_pairproduct_lean_largerput_heads_kernel(tc, query, keys_words, k
         a = sb.tile([P, T], F32, name="a")
         pieces = ((0, 512, "s"), (512, 256, "v"), (768, 128, "v"), (896, 128, "s"))
         for n, (t0, width, eng) in enumerate(pieces):
-            bank = ps.tile([P, width], F32, name=f"bank{n}")
+            bank = ps.tile([P, width], F32, name=f"bank{n}", tag=f"bank{n}")
             h, c0 = divmod(t0, HALF_T)
             nc.tensor.matmul_mx(
                 out=bank[:],
@@ -94,15 +98,33 @@ def tile_attend_pairproduct_lean_largerput_heads_kernel(tc, query, keys_words, k
                 nc.scalar.activation(right[:], a[:].indirect(list2[:, cols]), COPY)
             nc.vector.tensor_tensor(f1[:].indirect(list3[:, cols]), left[:], right[:], ALU.mult)
 
-        n_chunks = T // OUT_CHUNK
-        larger = [sb.tile([P, OUT_CHUNK], F32, name=f"larger{c}") for c in range(n_chunks)]
-        result = [sb.tile([P, OUT_CHUNK], F32, name=f"result{c}") for c in range(n_chunks)]
-        for step in range(n_chunks + 1):
-            if step < n_chunks:
-                cols = slice(step * OUT_CHUNK, (step + 1) * OUT_CHUNK)
-                nc.vector.tensor_tensor(larger[step][:], f1[:, cols], old_sb[:, cols], ALU.max)
-            if step > 0:
-                c = step - 1
-                cols = slice(c * OUT_CHUNK, (c + 1) * OUT_CHUNK)
-                nc.vector.scalar_tensor_tensor(result[c][:], old_sb[:, cols], 0.25, larger[c][:], ALU.mult, ALU.add)
-                nc.sync.dma_start(out=out[:, cols], in_=result[c][:])
+        old_ps = {}
+        for h, tag, factor in ((1, "bank2", 1.0), (0, "bank3", 1.25)):
+            turned_ps = ps.tile([P, HALF_T], F32, name=f"turned_ps{h}", tag=tag)
+            for b in range(HALF_T // P):
+                nc.tensor.transpose(turned_ps[:, b * P : (b + 1) * P], old_sb[:, h * HALF_T + b * P : h * HALF_T + (b + 1) * P], ident[:])
+            turned = sb.tile([P, HALF_T], F32, name=f"turned{h}")
+            nc.scalar.activation(turned[:], turned_ps[:], COPY, scale=factor)
+            back = ps.tile([P, HALF_T], F32, name=f"old_ps{h}")
+            for b in range(HALF_T // P):
+                nc.tensor.transpose(back[:, b * P : (b + 1) * P], turned[:, b * P : (b + 1) * P], ident[:])
+            old_ps[h] = back
+
+        first = [sb.tile([P, OUT_CHUNK], F32, name=f"first{c}") for c in range(4)]
+        result = [sb.tile([P, OUT_CHUNK], F32, name=f"result{c}") for c in range(4)]
+        for c in (0, 1):
+            cols = slice(c * OUT_CHUNK, (c + 1) * OUT_CHUNK)
+            nc.gpsimd.tensor_tensor(first[c][:], f1[:, cols], old_sb[:, cols], ALU.subtract)
+        for c in (2, 3):
+            cols = slice(c * OUT_CHUNK, (c + 1) * OUT_CHUNK)
+            local = slice((c - 2) * OUT_CHUNK, (c - 1) * OUT_CHUNK)
+            nc.vector.tensor_tensor(first[c][:], f1[:, cols], old_ps[1][:, local], ALU.max)
+        for c in (2, 3):
+            cols = slice(c * OUT_CHUNK, (c + 1) * OUT_CHUNK)
+            local = slice((c - 2) * OUT_CHUNK, (c - 1) * OUT_CHUNK)
+            nc.vector.scalar_tensor_tensor(result[c][:], old_ps[1][:, local], 0.25, first[c][:], ALU.mult, ALU.add)
+            nc.sync.dma_start(out=out[:, cols], in_=result[c][:])
+        for c in (0, 1):
+            cols = slice(c * OUT_CHUNK, (c + 1) * OUT_CHUNK)
+            nc.vector.scalar_tensor_tensor(result[c][:], first[c][:], 0.0, old_ps[0][:, cols], ALU.max, ALU.add)
+            nc.sync.dma_start(out=out[:, cols], in_=result[c][:])

@@ -64,8 +64,16 @@ def tile_attend_pairproduct_lean_largerput_heads_kernel(tc, query, keys_words, k
         q_bf = sb.tile([P, Q, PACK], BF16, name="q_bf", align_bytes=64)
         q_codes = sb.tile([P, Q], U32, name="q_codes", align_bytes=64)
         q_scales = sb.tile([P, Q], U8, name="q_scales", align_bytes=64)
-        nc.vector.tensor_copy(out=q_bf[:], in_=q_raw[:].rearrange("p j q -> p q j"))
-        nc.vector.quantize_mx(out=q_codes[:].bitcast(FP8X4), scales=q_scales[:], in_=q_bf[:].rearrange("p q j -> p (q j)"))
+        q_turned = q_raw[:].rearrange("p j q -> p q j")
+        nc.vector.tensor_copy(out=q_bf[:, 0:64, :], in_=q_turned[:, 0:64, :])
+        nc.vector.tensor_copy(out=q_bf[:, 64:96, :], in_=q_turned[:, 64:96, :])
+        nc.scalar.activation(q_bf[:, 96:128, :], q_turned[:, 96:128, :], COPY)
+        for q0 in (0, 64):
+            nc.vector.quantize_mx(
+                out=q_codes[:, q0 : q0 + 64].bitcast(FP8X4),
+                scales=q_scales[:, q0 : q0 + 64],
+                in_=q_bf[:, q0 : q0 + 64, :].rearrange("p q j -> p (q j)"),
+            )
 
         a = sb.tile([P, T], F32, name="a")
         pieces = ((0, 512, "s"), (512, 256, "v"), (768, 128, "v"), (896, 128, "s"))
@@ -98,33 +106,42 @@ def tile_attend_pairproduct_lean_largerput_heads_kernel(tc, query, keys_words, k
                 nc.scalar.activation(right[:], a[:].indirect(list2[:, cols]), COPY)
             nc.vector.tensor_tensor(f1[:].indirect(list3[:, cols]), left[:], right[:], ALU.mult)
 
-        old_ps = {}
-        for h, tag, factor in ((1, "bank2", 1.0), (0, "bank3", 1.25)):
-            turned_ps = ps.tile([P, HALF_T], F32, name=f"turned_ps{h}", tag=tag)
+        split = 640
+        old_ps = []
+        for h in range(2):
+            turned_ps = ps.tile([P, HALF_T], F32, name=f"turned_ps{h}", tag=f"bank{2 + h}")
             for b in range(HALF_T // P):
                 nc.tensor.transpose(turned_ps[:, b * P : (b + 1) * P], old_sb[:, h * HALF_T + b * P : h * HALF_T + (b + 1) * P], ident[:])
             turned = sb.tile([P, HALF_T], F32, name=f"turned{h}")
-            nc.scalar.activation(turned[:], turned_ps[:], COPY, scale=factor)
+            plain = min(HALF_T, split - h * HALF_T)
+            nc.scalar.activation(turned[:, :plain], turned_ps[:, :plain], COPY)
+            if plain < HALF_T:
+                nc.scalar.activation(turned[:, plain:], turned_ps[:, plain:], COPY, scale=1.25)
             back = ps.tile([P, HALF_T], F32, name=f"old_ps{h}")
             for b in range(HALF_T // P):
                 nc.tensor.transpose(back[:, b * P : (b + 1) * P], turned[:, b * P : (b + 1) * P], ident[:])
-            old_ps[h] = back
+            old_ps.append(back)
 
-        first = [sb.tile([P, OUT_CHUNK], F32, name=f"first{c}") for c in range(4)]
-        result = [sb.tile([P, OUT_CHUNK], F32, name=f"result{c}") for c in range(4)]
-        for c in (0, 1):
-            cols = slice(c * OUT_CHUNK, (c + 1) * OUT_CHUNK)
-            nc.gpsimd.tensor_tensor(first[c][:], f1[:, cols], old_sb[:, cols], ALU.subtract)
-        for c in (2, 3):
-            cols = slice(c * OUT_CHUNK, (c + 1) * OUT_CHUNK)
-            local = slice((c - 2) * OUT_CHUNK, (c - 1) * OUT_CHUNK)
-            nc.vector.tensor_tensor(first[c][:], f1[:, cols], old_ps[1][:, local], ALU.max)
-        for c in (2, 3):
-            cols = slice(c * OUT_CHUNK, (c + 1) * OUT_CHUNK)
-            local = slice((c - 2) * OUT_CHUNK, (c - 1) * OUT_CHUNK)
-            nc.vector.scalar_tensor_tensor(result[c][:], old_ps[1][:, local], 0.25, first[c][:], ALU.mult, ALU.add)
-            nc.sync.dma_start(out=out[:, cols], in_=result[c][:])
-        for c in (0, 1):
-            cols = slice(c * OUT_CHUNK, (c + 1) * OUT_CHUNK)
-            nc.vector.scalar_tensor_tensor(result[c][:], first[c][:], 0.0, old_ps[0][:, cols], ALU.max, ALU.add)
-            nc.sync.dma_start(out=out[:, cols], in_=result[c][:])
+        def in_psum(t0, t1):
+            h = t0 // HALF_T
+            return old_ps[h][:, t0 - h * HALF_T : t1 - h * HALF_T]
+
+        excess = sb.tile([P, T - split], F32, name="excess")
+        nc.gpsimd.tensor_tensor(excess[:], f1[:, split:], old_sb[:, split:], ALU.subtract)
+
+        queues = (nc.sync, nc.scalar)
+        own = ((0, 256), (256, 512), (512, split))
+        larger = [sb.tile([P, t1 - t0], F32, name=f"larger{t0}") for t0, t1 in own]
+        for step in range(len(own) + 1):
+            if step < len(own):
+                t0, t1 = own[step]
+                nc.vector.tensor_tensor(larger[step][:], f1[:, t0:t1], in_psum(t0, t1), ALU.max)
+            if step > 0:
+                t0, t1 = own[step - 1]
+                result = sb.tile([P, t1 - t0], F32, name=f"result{t0}")
+                nc.vector.scalar_tensor_tensor(result[:], in_psum(t0, t1), 0.25, larger[step - 1][:], ALU.mult, ALU.add)
+                queues[(step - 1) % 2].dma_start(out=out[:, t0:t1], in_=result[:])
+        for n, (t0, t1) in enumerate(((split, 896), (896, T))):
+            result = sb.tile([P, t1 - t0], F32, name=f"result{t0}")
+            nc.vector.scalar_tensor_tensor(result[:], excess[:, t0 - split : t1 - split], 0.0, in_psum(t0, t1), ALU.max, ALU.add)
+            queues[(len(own) + n) % 2].dma_start(out=out[:, t0:t1], in_=result[:])

from contextlib import ExitStack

import concourse.mybir as mybir
from concourse.masks import make_identity

D, T, I, Q = 512, 1024, 512, 128
FLOPS = 2 * D * T * Q

F32 = mybir.dt.float32
BF16 = mybir.dt.bfloat16
I32 = mybir.dt.int32
U32 = mybir.dt.uint32
U16 = mybir.dt.uint16
U8 = mybir.dt.uint8
FP8X4 = mybir.dt.float8_e4m3fn_x4
ALU = mybir.AluOpType
COPY = mybir.ActivationFunctionType.Copy

P = 128
PACK = 4
HALF_T = T // 2
HALF_I = I // 2
LIST_COLS = I // 16
OUT_CHUNK = 256


def tile_attend_pairproduct_lean_largerput_heads_kernel(tc, query, keys_words, keys_scales, old, offs, offs2, offs3, out):
    nc = tc.nc
    with ExitStack() as ctx:
        sb = ctx.enter_context(tc.tile_pool(name="sb", bufs=1))
        ps = ctx.enter_context(tc.psum_pool(name="ps", bufs=1))

        q_raw = sb.tile([P, PACK, Q], F32, name="q_raw")
        nc.sync.dma_start(out=q_raw[:], in_=query.rearrange("(p j) q -> p j q", j=PACK))

        k_scales = sb.tile([P, T], U8, name="k_scales", align_bytes=64)
        scale_rows = keys_scales[0].bitcast(I32)
        for quad in range(4):
            nc.sync.dma_start(out=k_scales[32 * quad : 32 * quad + 4, :].bitcast(I32), in_=scale_rows[4 * quad : 4 * quad + 4, :])

        word_rows = keys_words[0].rearrange("p t r -> p (t r)").bitcast(I32)
        k_words = []
        for h in range(2):
            kw = sb.tile([P, HALF_T], U32, name=f"k_words{h}", align_bytes=64)
            nc.sync.dma_start(out=kw[:].bitcast(I32), in_=word_rows[:, h * HALF_T : (h + 1) * HALF_T])
            k_words.append(kw)

        lists = []
        for name, src in (("list1", offs), ("list2", offs2), ("list3", offs3)):
            lt = sb.tile([P, LIST_COLS], U16, name=name)
            nc.sync.dma_start(lt[:], src)
            lists.append(lt)
        list1, list2, list3 = lists

        old_sb = sb.tile([P, T], F32, name="old_sb")
        nc.sync.dma_start(out=old_sb[:], in_=old)

        ident = sb.tile([P, P], F32, name="ident")
        make_identity(nc, ident[:])

        f1 = sb.tile([P, T], F32, name="f1")
        nc.vector.memset(f1[:], 0.0)

        q_bf = sb.tile([P, Q, PACK], BF16, name="q_bf", align_bytes=64)
        q_codes = sb.tile([P, Q], U32, name="q_codes", align_bytes=64)
        q_scales = sb.tile([P, Q], U8, name="q_scales", align_bytes=64)
        q_turned = q_raw[:].rearrange("p j q -> p q j")
        nc.vector.tensor_copy(out=q_bf[:, 0:64, :], in_=q_turned[:, 0:64, :])
        nc.vector.tensor_copy(out=q_bf[:, 64:96, :], in_=q_turned[:, 64:96, :])
        nc.scalar.activation(q_bf[:, 96:128, :], q_turned[:, 96:128, :], COPY)
        for q0 in (0, 64):
            nc.vector.quantize_mx(
                out=q_codes[:, q0 : q0 + 64].bitcast(FP8X4),
                scales=q_scales[:, q0 : q0 + 64],
                in_=q_bf[:, q0 : q0 + 64, :].rearrange("p q j -> p (q j)"),
            )

        a = sb.tile([P, T], F32, name="a")
        pieces = ((0, 512, "s"), (512, 256, "v"), (768, 128, "v"), (896, 128, "s"))
        for n, (t0, width, eng) in enumerate(pieces):
            bank = ps.tile([P, width], F32, name=f"bank{n}", tag=f"bank{n}")
            h, c0 = divmod(t0, HALF_T)
            nc.tensor.matmul_mx(
                out=bank[:],
                lhsT=q_codes[:].bitcast(FP8X4),
                lhsT_scale=q_scales[:],
                rhs=k_words[h][:, c0 : c0 + width].bitcast(FP8X4),
                rhs_scale=k_scales[:, t0 : t0 + width],
                start=True,
                stop=True,
            )
            if eng == "s":
                nc.scalar.activation(a[:, t0 : t0 + width], bank[:], COPY)
            else:
                nc.vector.tensor_copy(a[:, t0 : t0 + width], bank[:])

        half_cols = LIST_COLS // 2
        for h in range(2):
            cols = slice(h * half_cols, (h + 1) * half_cols)
            left = sb.tile([P, HALF_I], F32, name=f"left{h}")
            right = sb.tile([P, HALF_I], F32, name=f"right{h}")
            nc.scalar.activation(left[:], a[:].indirect(list1[:, cols]), COPY)
            if h == 0:
                nc.vector.tensor_copy(right[:], a[:].indirect(list2[:, cols]))
            else:
                nc.scalar.activation(right[:], a[:].indirect(list2[:, cols]), COPY)
            nc.vector.tensor_tensor(f1[:].indirect(list3[:, cols]), left[:], right[:], ALU.mult)

        split = 640
        old_ps = []
        for h in range(2):
            turned_ps = ps.tile([P, HALF_T], F32, name=f"turned_ps{h}", tag=f"bank{2 + h}")
            for b in range(HALF_T // P):
                nc.tensor.transpose(turned_ps[:, b * P : (b + 1) * P], old_sb[:, h * HALF_T + b * P : h * HALF_T + (b + 1) * P], ident[:])
            turned = sb.tile([P, HALF_T], F32, name=f"turned{h}")
            plain = min(HALF_T, split - h * HALF_T)
            nc.scalar.activation(turned[:, :plain], turned_ps[:, :plain], COPY)
            if plain < HALF_T:
                nc.scalar.activation(turned[:, plain:], turned_ps[:, plain:], COPY, scale=1.25)
            back = ps.tile([P, HALF_T], F32, name=f"old_ps{h}")
            for b in range(HALF_T // P):
                nc.tensor.transpose(back[:, b * P : (b + 1) * P], turned[:, b * P : (b + 1) * P], ident[:])
            old_ps.append(back)

        def in_psum(t0, t1):
            h = t0 // HALF_T
            return old_ps[h][:, t0 - h * HALF_T : t1 - h * HALF_T]

        excess = sb.tile([P, T - split], F32, name="excess")
        nc.gpsimd.tensor_tensor(excess[:], f1[:, split:], old_sb[:, split:], ALU.subtract)

        queues = (nc.sync, nc.scalar)
        own = ((0, 256), (256, 512), (512, split))
        larger = [sb.tile([P, t1 - t0], F32, name=f"larger{t0}") for t0, t1 in own]
        for step in range(len(own) + 1):
            if step < len(own):
                t0, t1 = own[step]
                nc.vector.tensor_tensor(larger[step][:], f1[:, t0:t1], in_psum(t0, t1), ALU.max)
            if step > 0:
                t0, t1 = own[step - 1]
                result = sb.tile([P, t1 - t0], F32, name=f"result{t0}")
                nc.vector.scalar_tensor_tensor(result[:], in_psum(t0, t1), 0.25, larger[step - 1][:], ALU.mult, ALU.add)
                queues[(step - 1) % 2].dma_start(out=out[:, t0:t1], in_=result[:])
        for n, (t0, t1) in enumerate(((split, 896), (896, T))):
            result = sb.tile([P, t1 - t0], F32, name=f"result{t0}")
            nc.vector.scalar_tensor_tensor(result[:], excess[:, t0 - split : t1 - split], 0.0, in_psum(t0, t1), ALU.max, ALU.add)
            queues[(len(own) + n) % 2].dma_start(out=out[:, t0:t1], in_=result[:])
